import numpy as np
import ml_dtypes


def mxq(x, axis, fmt="e4m3"):
    dtype, down = {"e4m3": (ml_dtypes.float8_e4m3fn, 7), "e5m2": (ml_dtypes.float8_e5m2, 14)}[fmt]
    v = np.moveaxis(np.asarray(x, np.float32).astype(ml_dtypes.bfloat16).astype(np.float64), axis, -1)
    blocks = v.reshape(v.shape[:-1] + (-1, 32))
    amax = np.abs(blocks).max(-1, keepdims=True)
    byte = np.maximum(np.where(amax > 0, np.frexp(amax)[1] - 1 + 127, 0) - down, 1)
    scale = np.exp2(byte - 127.0)
    codes = (blocks / scale).astype(np.float32).astype(dtype).astype(np.float64)
    return np.moveaxis((codes * scale).reshape(v.shape), -1, axis)


WIDE = False


def mx_kscale(k):
    if not WIDE:
        return np.ones(k)
    levels = np.array([10, -10, 5, -5, 0])
    if k % 512:
        return np.exp2(np.random.permutation(np.resize(levels, k // 32))).repeat(32)
    a = np.empty((k // 512, 16))
    for p in range(k // 512):
        a[p, :8] = np.random.permutation(np.resize(levels, 8))
        for g in range(8):
            far = levels[np.abs(levels - a[p, g]) >= 10]
            a[p, g + 8] = far[np.random.randint(len(far))]
    return np.exp2(a.ravel()).repeat(32)


def f64(x):
    return np.asarray(x).astype(np.float64)


def striped(idx):
    return np.tile(idx.reshape(-1, 16).T, (8, 1)).astype(np.uint16)


def unstriped(offs):
    return offs[:16].T.reshape(-1).astype(np.int64)


def pack_weight(w):
    k, n = w.shape
    w = f64(np.asarray(w, np.float32).astype(ml_dtypes.bfloat16)).reshape(k // 32, 32, n)
    amax = np.abs(w).max(1)
    byte = np.clip(np.where(amax > 0, np.frexp(amax)[1] - 1 + 127 - 7, 1), 1, 254)
    scaled = (w * np.exp2(127.0 - byte)[:, None, :]).reshape(k, n).astype(np.float32)
    words = np.ascontiguousarray(scaled.reshape(k // 512, 128, 4, n).transpose(0, 1, 3, 2)).astype(ml_dtypes.float8_e4m3fn).view(np.uint8)
    return words, np.ascontiguousarray(byte.astype(np.uint8).reshape(k // 512, 16, n))


def unpack_weight(words, scales):
    g, p, n, _ = words.shape
    vals = np.ascontiguousarray(words).view(ml_dtypes.float8_e4m3fn).astype(np.float64) * np.repeat(np.exp2(scales.astype(np.float64) - 127.0), 8, axis=1)[..., None]
    return vals.transpose(0, 1, 3, 2).reshape(g * 512, n)


def sigmoid(v):
    return 1.0 / (1.0 + np.exp(-np.maximum(v, -700.0)))


K, T, S, N, H, U = 512, 2048, 512, 128, 512, 1024


def setup_inputs():
    n = np.random.standard_normal
    s = mx_kscale(K)[:, None]
    u = mx_kscale(H)
    packed_xT = pack_weight(n((K, T)) * s)
    return {
        "x_words": packed_xT[0],
        "x_scales": packed_xT[1],
        "w1": (n((K, H)) / np.sqrt(K) / s).astype(np.float32),
        "w2": (n((K, H)) / np.sqrt(K) / s).astype(np.float32),
        "unit": (np.random.uniform(0.6, 1.4, (H, 1)) * u[:, None]).astype(np.float32),
        "w3": (n((H, N)) / np.sqrt(H) / u[:, None]).astype(np.float32),
        "offs": striped(np.random.permutation(T)[:S]),
        "h1": striped(np.random.permutation(np.concatenate([np.arange(S), np.random.randint(0, S, U - S)]))),
        "h2": striped(np.random.permutation(np.concatenate([np.arange(S), np.random.randint(0, S, U - S)]))),
        "h3": striped(np.random.permutation(np.concatenate([np.arange(S), np.random.randint(0, S, U - S)]))),
    }


def reference(x_words, x_scales, w1, w2, unit, w3, offs, h1, h2, h3):
    xq = unpack_weight(x_words, x_scales)[:, unstriped(offs)]
    y = mxq(f64(w1), 0, "e4m3").T @ xq
    bit = sigmoid(1.5 * y)
    b1 = bit[:, unstriped(h1)]
    b2 = bit[:, unstriped(h2)]
    b3 = bit[:, unstriped(h3)]
    memb = np.minimum(np.minimum(b1, b2), b3)
    yv = mxq(f64(w2), 0, "e4m3").T @ xq
    vh = yv[:, unstriped(h1)]
    hid = f64(unit) * (memb * vh)
    return mxq(f64(w3), 0, "e4m3").T @ mxq(hid, 0, "e4m3")

@@ -1,0 +1,176 @@
+from contextlib import ExitStack
+
+import concourse.mybir as mybir
+
+F32 = mybir.dt.float32
+BF16 = mybir.dt.bfloat16
+I32 = mybir.dt.int32
+U32 = mybir.dt.uint32
+U16 = mybir.dt.uint16
+U8 = mybir.dt.uint8
+FP8X4 = mybir.dt.float8_e4m3fn_x4
+MULT = mybir.AluOpType.mult
+MIN = mybir.AluOpType.min
+COPY = mybir.ActivationFunctionType.Copy
+SIGMOID = mybir.ActivationFunctionType.Sigmoid
+
+K, T, S, N, H, U = 512, 2048, 512, 128, 512, 1024
+P = 128
+PACK = 4
+GROUP = 16
+CHUNKS = (384, 384, 256)
+VECTOR_THIRD = 4
+FLOPS = 2 * (2 * K * H * S + H * N * U)
+
+
+def tile_picked_ybloomj_join_p_kernel(tc, x_words, x_scales, w1, w2, unit, w3, offs, h1, h2, h3, out):
+    nc = tc.nc
+    with ExitStack() as ctx:
+        lists = ctx.enter_context(tc.tile_pool(name="lists", bufs=1))
+        keep = ctx.enter_context(tc.tile_pool(name="keep", bufs=1))
+        psum = ctx.enter_context(tc.psum_pool(name="psum", bufs=8))
+
+        def load_list(name, src):
+            tile = lists.tile(list(src.shape), U16, name=name)
+            nc.sync.dma_start(tile[:], src)
+            return tile
+
+        def load_rows(name, src):
+            tile = keep.tile([P, PACK, src.shape[1]], F32, name=name)
+            nc.sync.dma_start(tile[:], src.rearrange("(p j) c -> p j c", j=PACK))
+            return tile
+
+        def quantize(name, grouped, width):
+            codes = keep.tile([P, width], U32, name=name + "_codes", align_bytes=64)
+            scales = keep.tile([P, width], U8, name=name + "_scales", align_bytes=64)
+            nc.vector.quantize_mx(out=codes[:].bitcast(FP8X4), scales=scales[:], in_=grouped)
+            return codes, scales
+
+        def deal(name, raw, pair, copy):
+            grouped = keep.tile([P, 2, P, PACK], BF16, name=name, align_bytes=64)
+            copy(
+                grouped[:].rearrange("p t m j -> p m j t"),
+                raw[:].rearrange("p j (m t) -> p m j t", t=PACK)[:, :, :, 2 * pair : 2 * pair + 2],
+            )
+            return grouped[:].rearrange("p t m j -> p (t m j)")
+
+        def product(acc, lhs, lhs_cols, rhs, rhs_cols):
+            nc.tensor.matmul_mx(
+                out=acc,
+                lhsT=lhs[0][:, lhs_cols].bitcast(FP8X4),
+                lhsT_scale=lhs[1][:, lhs_cols],
+                rhs=rhs[0][:, rhs_cols].bitcast(FP8X4),
+                rhs_scale=rhs[1][:, rhs_cols],
+                start=True,
+                stop=True,
+            )
+
+        table_scales = keep.tile([P, T], U8, name="table_scales")
+        nc.vector.memset(table_scales[:].bitcast(I32), 0)
+
+        w1_raw = load_rows("w1_raw", w1)
+        offs_sb = load_list("offs_sb", offs)
+        for q in range(4):
+            nc.sync.dma_start(table_scales[32 * q : 32 * q + 4, :].bitcast(I32), x_scales[0, 4 * q : 4 * q + 4, :].bitcast(I32))
+        table_words = keep.tile([P, T], I32, name="table_words")
+        nc.sync.dma_start(table_words[:], x_words[0].rearrange("p c r -> p (c r)").bitcast(I32))
+        h1_sb = load_list("h1_sb", h1)
+        h2_sb = load_list("h2_sb", h2)
+        h3_sb = load_list("h3_sb", h3)
+        w2_raw = load_rows("w2_raw", w2)
+        unit_sb = keep.tile([P, PACK], F32, name="unit_sb")
+        nc.sync.dma_start(unit_sb[:], unit.rearrange("(p t) o -> p (t o)", t=PACK))
+        w3_raw = load_rows("w3_raw", w3)
+
+        w1_dealt = [deal("w1_low", w1_raw, 0, nc.vector.tensor_copy), deal("w1_high", w1_raw, 1, nc.scalar.copy)]
+        x_bytes = keep.tile([P, S], U8, name="x_bytes", align_bytes=64)
+        nc.vector.tensor_copy(x_bytes[:], table_scales[:].indirect(offs_sb[:]))
+        w1_q = [quantize("w1_%d" % u, w1_dealt[u], 2 * P) for u in range(2)]
+        x_codes = keep.tile([P, S], U32, name="x_codes", align_bytes=64)
+        nc.vector.tensor_copy(x_codes[:], table_words[:].bitcast(U32).indirect(offs_sb[:]))
+        x_q = (x_codes, x_bytes)
+
+        def first_product(w_q, t):
+            acc = psum.tile([P, S], F32, tag="acc", name="acc")
+            product(acc[:], w_q[t // 2], slice(P * (t % 2), P * (t % 2 + 1)), x_q, slice(0, S))
+            return acc
+
+        y = [first_product(w1_q, t) for t in range(PACK)]
+
+        starts = [sum(CHUNKS[:c]) for c in range(len(CHUNKS))]
+        steps = [(c, t) for c in range(len(CHUNKS)) for t in range(PACK)]
+        bit, value, yv, fetched, hid, grouped = {}, {}, {}, {}, {}, {}
+        w3_q = []
+
+        def entries(tile, c):
+            return tile[:, starts[c] // GROUP : (starts[c] + CHUNKS[c]) // GROUP]
+
+        def fetch(s):
+            c, t = steps[s]
+            if c == 0:
+                bit[t] = keep.tile([P, S], F32, name="bit%d" % t)
+                nc.scalar.activation(bit[t][:], y[t][:], SIGMOID, scale=1.5)
+            fetched[s] = [keep.tile([P, CHUNKS[c]], F32, name="b%d_%d" % (i, s)) for i in range(3)]
+            for i, tile in enumerate((h1_sb, h2_sb, h3_sb)):
+                window = bit[t][:].indirect(entries(tile, c))
+                if i == 2 and s < VECTOR_THIRD:
+                    nc.vector.tensor_copy(fetched[s][i][:], window)
+                else:
+                    nc.scalar.activation(fetched[s][i][:], window, COPY)
+
+        def smaller(s, i):
+            nc.vector.tensor_tensor(fetched[s][0][:], fetched[s][0][:], fetched[s][i][:], MIN)
+
+        def let_through(s):
+            c, t = steps[s]
+            if c == 0:
+                value[t] = keep.tile([P, S], F32, name="value%d" % t)
+                nc.vector.tensor_scalar(value[t][:], yv[t][:], unit_sb[:, t : t + 1], None, MULT)
+            if t == 0:
+                hid[c] = keep.tile([P, PACK, CHUNKS[c]], F32, name="hid%d" % c)
+            nc.vector.tensor_tensor(hid[c][:, t, :], value[t][:].indirect(entries(h1_sb, c)), fetched[s][0][:], MULT)
+
+        def interleave(name, rows, width):
+            tile = keep.tile([P, width, PACK], BF16, name=name, align_bytes=64)
+            nc.vector.tensor_copy(
+                tile[:].rearrange("p (c i) t -> p c t i", i=4),
+                rows[:].rearrange("p t (c i) -> p c t i", i=4),
+            )
+            return tile[:].rearrange("p c t -> p (c t)")
+
+        def last_product(c):
+            width = CHUNKS[c]
+            hid_q = quantize("hid_%d" % c, grouped[c], width)
+            acc = psum.tile([P, S], F32, tag="acc", name="acc")
+            done = 0
+            for piece in (256, 128):
+                while width - done >= piece:
+                    product(acc[:, done : done + piece], w3_q[0], slice(0, N), hid_q, slice(done, done + piece))
+                    done = done + piece
+            result = keep.tile([P, width], F32, name="result%d" % c)
+            nc.scalar.copy(result[:], acc[:, :width])
+            nc.sync.dma_start(out[:, starts[c] : starts[c] + width], result[:])
+
+        for s in range(len(steps) + 4):
+            if s < len(steps):
+                fetch(s)
+            if s == 0:
+                w2_dealt = [deal("w2_%d" % u, w2_raw, u, nc.vector.tensor_copy) for u in range(2)]
+                w2_q = [quantize("w2_%d" % u, w2_dealt[u], 2 * P) for u in range(2)]
+                for t in range(PACK):
+                    yv[t] = first_product(w2_q, t)
+            if s == 1:
+                w3_grouped = interleave("w3_grouped", w3_raw, N)
+            if s == 2:
+                w3_q.append(quantize("w3", w3_grouped, N))
+            if s < len(steps):
+                smaller(s, 1)
+            if 0 <= s - 4 < len(steps) and steps[s - 4][1] == PACK - 1:
+                last_product(steps[s - 4][0])
+            if 0 <= s - 1 < len(steps):
+                smaller(s - 1, 2)
+            if 0 <= s - 3 < len(steps) and steps[s - 3][1] == PACK - 1:
+                c = steps[s - 3][0]
+                grouped[c] = interleave("grouped%d" % c, hid[c], CHUNKS[c])
+            if 0 <= s - 2 < len(steps):
+                let_through(s - 2)

@@ -18,8 +18,10 @@ K, T, S, N, H, U = 512, 2048, 512, 128, 512, 1024
 P = 128
 PACK = 4
 GROUP = 16
-CHUNKS = (384, 384, 256)
+CHUNKS = (512, 256, 256)
 VECTOR_THIRD = 4
+MERGE = (1, 4, 4)
+WINDOW = S + GROUP
 FLOPS = 2 * (2 * K * H * S + H * N * U)
 
 
@@ -68,67 +70,75 @@ def tile_picked_ybloomj_join_p_kernel(tc, x_words, x_scales, w1, w2, unit, w3, o
         table_scales = keep.tile([P, T], U8, name="table_scales")
         nc.vector.memset(table_scales[:].bitcast(I32), 0)
 
-        w1_raw = load_rows("w1_raw", w1)
+        bit = [keep.tile([P, WINDOW], F32, name="bit%d" % t) for t in range(PACK)]
+        value = [keep.tile([P, WINDOW], F32, name="value%d" % t) for t in range(PACK)]
+        for tile in bit + value:
+            nc.vector.memset(tile[:, S:], 0.0)
+
         offs_sb = load_list("offs_sb", offs)
         for q in range(4):
-            nc.sync.dma_start(table_scales[32 * q : 32 * q + 4, :].bitcast(I32), x_scales[0, 4 * q : 4 * q + 4, :].bitcast(I32))
+            nc.sync.dma_start(table_scales[q:P:32, :].bitcast(I32), x_scales[0, q:16:4, :].bitcast(I32))
+        w1_raw = load_rows("w1_raw", w1)
         table_words = keep.tile([P, T], I32, name="table_words")
         nc.sync.dma_start(table_words[:], x_words[0].rearrange("p c r -> p (c r)").bitcast(I32))
         h1_sb = load_list("h1_sb", h1)
         h2_sb = load_list("h2_sb", h2)
         h3_sb = load_list("h3_sb", h3)
+        w3_raw = load_rows("w3_raw", w3)
         w2_raw = load_rows("w2_raw", w2)
         unit_sb = keep.tile([P, PACK], F32, name="unit_sb")
         nc.sync.dma_start(unit_sb[:], unit.rearrange("(p t) o -> p (t o)", t=PACK))
-        w3_raw = load_rows("w3_raw", w3)
 
-        w1_dealt = [deal("w1_low", w1_raw, 0, nc.vector.tensor_copy), deal("w1_high", w1_raw, 1, nc.scalar.copy)]
         x_bytes = keep.tile([P, S], U8, name="x_bytes", align_bytes=64)
         nc.vector.tensor_copy(x_bytes[:], table_scales[:].indirect(offs_sb[:]))
+        w1_dealt = [deal("w1_low", w1_raw, 0, nc.vector.tensor_copy), deal("w1_high", w1_raw, 1, nc.vector.tensor_copy)]
         w1_q = [quantize("w1_%d" % u, w1_dealt[u], 2 * P) for u in range(2)]
         x_codes = keep.tile([P, S], U32, name="x_codes", align_bytes=64)
-        nc.vector.tensor_copy(x_codes[:], table_words[:].bitcast(U32).indirect(offs_sb[:]))
+        halves = [slice(0, S // 2), slice(S // 2, S)]
+        for half in halves:
+            picked = offs_sb[:, half.start // GROUP : half.stop // GROUP]
+            nc.vector.tensor_copy(x_codes[:, half], table_words[:].bitcast(U32).indirect(picked))
         x_q = (x_codes, x_bytes)
 
-        def first_product(w_q, t):
+        def first_product(w_q, t, cols):
             acc = psum.tile([P, S], F32, tag="acc", name="acc")
-            product(acc[:], w_q[t // 2], slice(P * (t % 2), P * (t % 2 + 1)), x_q, slice(0, S))
+            product(acc[:, cols], w_q[t // 2], slice(P * (t % 2), P * (t % 2 + 1)), x_q, cols)
             return acc
 
-        y = [first_product(w1_q, t) for t in range(PACK)]
+        y = [[(first_product(w1_q, t, cols), cols) for cols in (halves if t == 0 else [slice(0, S)])] for t in range(PACK)]
 
         starts = [sum(CHUNKS[:c]) for c in range(len(CHUNKS))]
-        steps = [(c, t) for c in range(len(CHUNKS)) for t in range(PACK)]
-        bit, value, yv, fetched, hid, grouped = {}, {}, {}, {}, {}, {}
+        steps = [(c, range(t, t + MERGE[c])) for c in range(len(CHUNKS)) for t in range(0, PACK, MERGE[c])]
+        yv, fetched, hid, grouped, sums = {}, {}, {}, {}, {}
         w3_q = []
 
         def entries(tile, c):
             return tile[:, starts[c] // GROUP : (starts[c] + CHUNKS[c]) // GROUP]
 
         def fetch(s):
-            c, t = steps[s]
+            c, tiles = steps[s]
+            fetched[s] = [keep.tile([P, len(tiles), CHUNKS[c]], F32, name="b%d_%d" % (i, s)) for i in range(3)]
             if c == 0:
-                bit[t] = keep.tile([P, S], F32, name="bit%d" % t)
-                nc.scalar.activation(bit[t][:], y[t][:], SIGMOID, scale=1.5)
-            fetched[s] = [keep.tile([P, CHUNKS[c]], F32, name="b%d_%d" % (i, s)) for i in range(3)]
+                for t in tiles:
+                    for acc, cols in y[t]:
+                        nc.scalar.activation(bit[t][:, cols], acc[:, cols], SIGMOID, scale=1.5)
             for i, tile in enumerate((h1_sb, h2_sb, h3_sb)):
-                window = bit[t][:].indirect(entries(tile, c))
-                if i == 2 and s < VECTOR_THIRD:
-                    nc.vector.tensor_copy(fetched[s][i][:], window)
-                else:
-                    nc.scalar.activation(fetched[s][i][:], window, COPY)
+                for t in tiles:
+                    window = bit[t][:].indirect(entries(tile, c))
+                    if i == 2 and PACK * c + t < VECTOR_THIRD:
+                        nc.vector.tensor_copy(fetched[s][i][:, t - tiles.start, :], window)
+                    else:
+                        nc.scalar.activation(fetched[s][i][:, t - tiles.start, :], window, COPY)
 
         def smaller(s, i):
             nc.vector.tensor_tensor(fetched[s][0][:], fetched[s][0][:], fetched[s][i][:], MIN)
 
         def let_through(s):
-            c, t = steps[s]
-            if c == 0:
-                value[t] = keep.tile([P, S], F32, name="value%d" % t)
-                nc.vector.tensor_scalar(value[t][:], yv[t][:], unit_sb[:, t : t + 1], None, MULT)
-            if t == 0:
+            c, tiles = steps[s]
+            if tiles.start == 0:
                 hid[c] = keep.tile([P, PACK, CHUNKS[c]], F32, name="hid%d" % c)
-            nc.vector.tensor_tensor(hid[c][:, t, :], value[t][:].indirect(entries(h1_sb, c)), fetched[s][0][:], MULT)
+            for t in tiles:
+                nc.vector.tensor_tensor(hid[c][:, t, :], value[t][:].indirect(entries(h1_sb, c)), fetched[s][0][:, t - tiles.start, :], MULT)
 
         def interleave(name, rows, width):
             tile = keep.tile([P, width, PACK], BF16, name=name, align_bytes=64)
@@ -143,34 +153,63 @@ def tile_picked_ybloomj_join_p_kernel(tc, x_words, x_scales, w1, w2, unit, w3, o
             hid_q = quantize("hid_%d" % c, grouped[c], width)
             acc = psum.tile([P, S], F32, tag="acc", name="acc")
             done = 0
-            for piece in (256, 128):
-                while width - done >= piece:
+            for piece in (512, 256, 128):
+                if width - done >= piece:
                     product(acc[:, done : done + piece], w3_q[0], slice(0, N), hid_q, slice(done, done + piece))
                     done = done + piece
+            sums[c] = acc
+
+        def store(c):
+            width = CHUNKS[c]
             result = keep.tile([P, width], F32, name="result%d" % c)
-            nc.scalar.copy(result[:], acc[:, :width])
+            nc.scalar.copy(result[:], sums[c][:, :width])
             nc.sync.dma_start(out[:, starts[c] : starts[c] + width], result[:])
 
-        for s in range(len(steps) + 4):
-            if s < len(steps):
-                fetch(s)
+        def closes(s):
+            return 0 <= s < len(steps) and steps[s][1].stop == PACK
+
+        w3_q.append(quantize("w3", interleave("w3_grouped", w3_raw, N), N))
+        last = len(steps) - 1
+        for s in range(last):
+            fetch(s)
             if s == 0:
                 w2_dealt = [deal("w2_%d" % u, w2_raw, u, nc.vector.tensor_copy) for u in range(2)]
                 w2_q = [quantize("w2_%d" % u, w2_dealt[u], 2 * P) for u in range(2)]
                 for t in range(PACK):
-                    yv[t] = first_product(w2_q, t)
-            if s == 1:
-                w3_grouped = interleave("w3_grouped", w3_raw, N)
-            if s == 2:
-                w3_q.append(quantize("w3", w3_grouped, N))
-            if s < len(steps):
-                smaller(s, 1)
-            if 0 <= s - 4 < len(steps) and steps[s - 4][1] == PACK - 1:
-                last_product(steps[s - 4][0])
-            if 0 <= s - 1 < len(steps):
-                smaller(s - 1, 2)
-            if 0 <= s - 3 < len(steps) and steps[s - 3][1] == PACK - 1:
-                c = steps[s - 3][0]
+                    yv[t] = first_product(w2_q, t, slice(0, S))
+            if closes(s - 2):
+                last_product(steps[s - 2][0])
+            if s > 0:
+                let_through(s - 1)
+            smaller(s, 1)
+            if closes(s - 1):
+                c = steps[s - 1][0]
                 grouped[c] = interleave("grouped%d" % c, hid[c], CHUNKS[c])
-            if 0 <= s - 2 < len(steps):
-                let_through(s - 2)
+            if steps[s][0] == 0:
+                for t in steps[s][1]:
+                    nc.vector.tensor_scalar(value[t][:, :S], yv[t][:], unit_sb[:, t : t + 1], None, MULT)
+            smaller(s, 2)
+
+        c = steps[last][0]
+        fetch(last)
+        vh = keep.tile([P, PACK, CHUNKS[c]], F32, name="vh")
+        for t in range(PACK):
+            nc.scalar.activation(vh[:, t, :], value[t][:].indirect(entries(h1_sb, c)), COPY)
+        if closes(last - 2):
+            last_product(steps[last - 2][0])
+        let_through(last - 1)
+        grouped[c - 1] = interleave("grouped%d" % (c - 1), hid[c - 1], CHUNKS[c - 1])
+        smaller(last, 1)
+        last_product(c - 1)
+        smaller(last, 2)
+        tile = keep.tile([P, CHUNKS[c], PACK], BF16, name="grouped_last", align_bytes=64)
+        nc.vector.tensor_tensor(
+            tile[:].rearrange("p (c i) t -> p c t i", i=4),
+            vh[:].rearrange("p t (c i) -> p c t i", i=4),
+            fetched[last][0][:].rearrange("p t (c i) -> p c t i", i=4),
+            MULT,
+        )
+        grouped[c] = tile[:].rearrange("p c t -> p (c t)")
+        last_product(c)
+        for c in range(len(CHUNKS)):
+            store(c)

@@ -18,10 +18,12 @@ K, T, S, N, H, U = 512, 2048, 512, 128, 512, 1024
 P = 128
 PACK = 4
 GROUP = 16
-CHUNKS = (512, 256, 256)
-VECTOR_THIRD = 4
-MERGE = (1, 4, 4)
-WINDOW = S + GROUP
+CHUNKS = (768, 256)
+VECTOR_THIRD = 3
+SCALAR_VALUES = 0
+TAIL = (128, 128)
+MERGE = (1, 4)
+WINDOW = max(CHUNKS) + GROUP
 FLOPS = 2 * (2 * K * H * S + H * N * U)
 
 
@@ -109,7 +111,7 @@ def tile_picked_ybloomj_join_p_kernel(tc, x_words, x_scales, w1, w2, unit, w3, o
 
         starts = [sum(CHUNKS[:c]) for c in range(len(CHUNKS))]
         steps = [(c, range(t, t + MERGE[c])) for c in range(len(CHUNKS)) for t in range(0, PACK, MERGE[c])]
-        yv, fetched, hid, grouped, sums = {}, {}, {}, {}, {}
+        yv, fetched, hid, grouped, sums = {}, {}, {}, {}, []
         w3_q = []
 
         def entries(tile, c):
@@ -122,13 +124,13 @@ def tile_picked_ybloomj_join_p_kernel(tc, x_words, x_scales, w1, w2, unit, w3, o
                 for t in tiles:
                     for acc, cols in y[t]:
                         nc.scalar.activation(bit[t][:, cols], acc[:, cols], SIGMOID, scale=1.5)
-            for i, tile in enumerate((h1_sb, h2_sb, h3_sb)):
-                for t in tiles:
-                    window = bit[t][:].indirect(entries(tile, c))
-                    if i == 2 and PACK * c + t < VECTOR_THIRD:
-                        nc.vector.tensor_copy(fetched[s][i][:, t - tiles.start, :], window)
-                    else:
-                        nc.scalar.activation(fetched[s][i][:, t - tiles.start, :], window, COPY)
+            order = [(i, t) for first in tiles[::2] for i in range(2) for t in range(first, min(first + 2, tiles.stop))]
+            for i, t in order + [(2, t) for t in tiles]:
+                window = bit[t][:].indirect(entries((h1_sb, h2_sb, h3_sb)[i], c))
+                if i == 2 and PACK * c + t < VECTOR_THIRD:
+                    nc.vector.tensor_copy(fetched[s][i][:, t - tiles.start, :], window)
+                else:
+                    nc.scalar.activation(fetched[s][i][:, t - tiles.start, :], window, COPY)
 
         def smaller(s, i):
             nc.vector.tensor_tensor(fetched[s][0][:], fetched[s][0][:], fetched[s][i][:], MIN)
@@ -148,22 +150,25 @@ def tile_picked_ybloomj_join_p_kernel(tc, x_words, x_scales, w1, w2, unit, w3, o
             )
             return tile[:].rearrange("p c t -> p (c t)")
 
-        def last_product(c):
-            width = CHUNKS[c]
-            hid_q = quantize("hid_%d" % c, grouped[c], width)
-            acc = psum.tile([P, S], F32, tag="acc", name="acc")
-            done = 0
-            for piece in (512, 256, 128):
-                if width - done >= piece:
-                    product(acc[:, done : done + piece], w3_q[0], slice(0, N), hid_q, slice(done, done + piece))
-                    done = done + piece
-            sums[c] = acc
+        def last_product(source, start, width):
+            for first in range(0, width, S):
+                piece = min(S, width - first)
+                hid_q = quantize("hid_%d" % (start + first), source[:, PACK * first : PACK * (first + piece)], piece)
+                acc = psum.tile([P, S], F32, tag="acc", name="acc")
+                done = 0
+                for run in (512, 256, 128):
+                    if piece - done >= run:
+                        product(acc[:, done : done + run], w3_q[0], slice(0, N), hid_q, slice(done, done + run))
+                        done = done + run
+                sums.append((acc, start + first, piece))
 
-        def store(c):
-            width = CHUNKS[c]
-            result = keep.tile([P, width], F32, name="result%d" % c)
-            nc.scalar.copy(result[:], sums[c][:, :width])
-            nc.sync.dma_start(out[:, starts[c] : starts[c] + width], result[:])
+        def store(acc, start, width, queue):
+            result = keep.tile([P, width], F32, name="result%d" % start)
+            nc.scalar.copy(result[:], acc[:, :width])
+            queue.dma_start(out[:, start : start + width], result[:])
+
+        def close(c):
+            last_product(grouped[c], starts[c], CHUNKS[c])
 
         def closes(s):
             return 0 <= s < len(steps) and steps[s][1].stop == PACK
@@ -178,7 +183,7 @@ def tile_picked_ybloomj_join_p_kernel(tc, x_words, x_scales, w1, w2, unit, w3, o
                 for t in range(PACK):
                     yv[t] = first_product(w2_q, t, slice(0, S))
             if closes(s - 2):
-                last_product(steps[s - 2][0])
+                close(steps[s - 2][0])
             if s > 0:
                 let_through(s - 1)
             smaller(s, 1)
@@ -187,29 +192,40 @@ def tile_picked_ybloomj_join_p_kernel(tc, x_words, x_scales, w1, w2, unit, w3, o
                 grouped[c] = interleave("grouped%d" % c, hid[c], CHUNKS[c])
             if steps[s][0] == 0:
                 for t in steps[s][1]:
-                    nc.vector.tensor_scalar(value[t][:, :S], yv[t][:], unit_sb[:, t : t + 1], None, MULT)
+                    if t < PACK - SCALAR_VALUES:
+                        nc.vector.tensor_scalar(value[t][:, :S], yv[t][:], unit_sb[:, t : t + 1], None, MULT)
+                    else:
+                        nc.scalar.activation(value[t][:, :S], yv[t][:], COPY, scale=unit_sb[:, t : t + 1])
             smaller(s, 2)
 
         c = steps[last][0]
         fetch(last)
-        vh = keep.tile([P, PACK, CHUNKS[c]], F32, name="vh")
-        for t in range(PACK):
-            nc.scalar.activation(vh[:, t, :], value[t][:].indirect(entries(h1_sb, c)), COPY)
+        parts = [(sum(TAIL[:j]), TAIL[j]) for j in range(len(TAIL))]
+        vh = []
+        for first, width in parts:
+            vh.append(keep.tile([P, PACK, width], F32, name="vh%d" % first))
+            for t in range(PACK):
+                picked = h1_sb[:, (starts[c] + first) // GROUP : (starts[c] + first + width) // GROUP]
+                nc.scalar.activation(vh[-1][:, t, :], value[t][:].indirect(picked), COPY)
         if closes(last - 2):
-            last_product(steps[last - 2][0])
+            close(steps[last - 2][0])
         let_through(last - 1)
         grouped[c - 1] = interleave("grouped%d" % (c - 1), hid[c - 1], CHUNKS[c - 1])
-        smaller(last, 1)
-        last_product(c - 1)
+        for pair in (slice(0, 2), slice(2, 4)):
+            nc.vector.tensor_tensor(fetched[last][0][:, pair, :], fetched[last][0][:, pair, :], fetched[last][1][:, pair, :], MIN)
+        close(c - 1)
         smaller(last, 2)
-        tile = keep.tile([P, CHUNKS[c], PACK], BF16, name="grouped_last", align_bytes=64)
-        nc.vector.tensor_tensor(
-            tile[:].rearrange("p (c i) t -> p c t i", i=4),
-            vh[:].rearrange("p t (c i) -> p c t i", i=4),
-            fetched[last][0][:].rearrange("p t (c i) -> p c t i", i=4),
-            MULT,
-        )
-        grouped[c] = tile[:].rearrange("p c t -> p (c t)")
-        last_product(c)
-        for c in range(len(CHUNKS)):
-            store(c)
+        tails = []
+        for (first, width), values in zip(parts, vh):
+            tile = keep.tile([P, width, PACK], BF16, name="grouped_last%d" % first, align_bytes=64)
+            nc.vector.tensor_tensor(
+                tile[:].rearrange("p (c i) t -> p c t i", i=4),
+                values[:].rearrange("p t (c i) -> p c t i", i=4),
+                fetched[last][0][:, :, first : first + width].rearrange("p t (c i) -> p c t i", i=4),
+                MULT,
+            )
+            tails.append(tile[:].rearrange("p c t -> p (c t)"))
+        for (first, width), source in zip(parts, tails):
+            last_product(source, starts[c] + first, width)
+        for acc, start, width in sums:
+            store(acc, start, width, nc.sync)

@@ -15,16 +15,20 @@ COPY = mybir.ActivationFunctionType.Copy
 SIGMOID = mybir.ActivationFunctionType.Sigmoid
 
 K, T, S, N, H, U = 512, 2048, 512, 128, 512, 1024
+FLOPS = 2 * (2 * K * H * S + H * N * U)
+
 P = 128
 PACK = 4
+QUADRANT = 32
 GROUP = 16
-CHUNKS = (768, 256)
-VECTOR_THIRD = 3
-SCALAR_VALUES = 0
-TAIL = (128, 128)
-MERGE = (1, 4)
-WINDOW = max(CHUNKS) + GROUP
-FLOPS = 2 * (2 * K * H * S + H * N * U)
+BANK = 512
+LINE = 4
+WIDE = 768
+NARROW = U - WIDE
+PART = 128
+WINDOW = WIDE + GROUP
+VECTOR_H3 = 3
+VECTOR_VALUES = 3
 
 
 def tile_picked_ybloomj_join_p_kernel(tc, x_words, x_scales, w1, w2, unit, w3, offs, h1, h2, h3, out):
@@ -44,23 +48,34 @@ def tile_picked_ybloomj_join_p_kernel(tc, x_words, x_scales, w1, w2, unit, w3, o
             nc.sync.dma_start(tile[:], src.rearrange("(p j) c -> p j c", j=PACK))
             return tile
 
-        def quantize(name, grouped, width):
-            codes = keep.tile([P, width], U32, name=name + "_codes", align_bytes=64)
-            scales = keep.tile([P, width], U8, name=name + "_scales", align_bytes=64)
-            nc.vector.quantize_mx(out=codes[:].bitcast(FP8X4), scales=scales[:], in_=grouped)
-            return codes, scales
+        def entries(list_tile, start, count):
+            return list_tile[:, start // GROUP : (start + count) // GROUP]
 
-        def deal(name, raw, pair, copy):
+        def quantize(name, grouped, width):
+            words = keep.tile([P, width], U32, name=name + "_words", align_bytes=64)
+            scales = keep.tile([P, width], U8, name=name + "_scales", align_bytes=64)
+            nc.vector.quantize_mx(out=words[:].bitcast(FP8X4), scales=scales[:], in_=grouped)
+            return words, scales
+
+        def deal(name, raw, pair):
             grouped = keep.tile([P, 2, P, PACK], BF16, name=name, align_bytes=64)
-            copy(
+            nc.vector.tensor_copy(
                 grouped[:].rearrange("p t m j -> p m j t"),
                 raw[:].rearrange("p j (m t) -> p m j t", t=PACK)[:, :, :, 2 * pair : 2 * pair + 2],
             )
             return grouped[:].rearrange("p t m j -> p (t m j)")
 
-        def product(acc, lhs, lhs_cols, rhs, rhs_cols):
+        def by_lines(rows):
+            return rows.rearrange("p t (c i) -> p c t i", i=LINE)
+
+        def interleaved(name, width):
+            tile = keep.tile([P, width, PACK], BF16, name=name, align_bytes=64)
+            return tile[:].rearrange("p (c i) t -> p c t i", i=LINE), tile[:].rearrange("p c t -> p (c t)")
+
+        def product(lhs, lhs_cols, rhs, rhs_cols, acc_cols):
+            acc = psum.tile([P, BANK], F32, tag="acc", name="acc")
             nc.tensor.matmul_mx(
-                out=acc,
+                out=acc[:, acc_cols],
                 lhsT=lhs[0][:, lhs_cols].bitcast(FP8X4),
                 lhsT_scale=lhs[1][:, lhs_cols],
                 rhs=rhs[0][:, rhs_cols].bitcast(FP8X4),
@@ -68,24 +83,22 @@ def tile_picked_ybloomj_join_p_kernel(tc, x_words, x_scales, w1, w2, unit, w3, o
                 start=True,
                 stop=True,
             )
+            return acc[:, acc_cols]
 
         table_scales = keep.tile([P, T], U8, name="table_scales")
         nc.vector.memset(table_scales[:].bitcast(I32), 0)
-
         bit = [keep.tile([P, WINDOW], F32, name="bit%d" % t) for t in range(PACK)]
         value = [keep.tile([P, WINDOW], F32, name="value%d" % t) for t in range(PACK)]
         for tile in bit + value:
             nc.vector.memset(tile[:, S:], 0.0)
 
         offs_sb = load_list("offs_sb", offs)
-        for q in range(4):
-            nc.sync.dma_start(table_scales[q:P:32, :].bitcast(I32), x_scales[0, q:16:4, :].bitcast(I32))
+        for r in range(PACK):
+            nc.sync.dma_start(table_scales[r:P:QUADRANT, :].bitcast(I32), x_scales[0, r : K // 32 : PACK, :].bitcast(I32))
         w1_raw = load_rows("w1_raw", w1)
         table_words = keep.tile([P, T], I32, name="table_words")
         nc.sync.dma_start(table_words[:], x_words[0].rearrange("p c r -> p (c r)").bitcast(I32))
-        h1_sb = load_list("h1_sb", h1)
-        h2_sb = load_list("h2_sb", h2)
-        h3_sb = load_list("h3_sb", h3)
+        h_sb = [load_list("h1_sb", h1), load_list("h2_sb", h2), load_list("h3_sb", h3)]
         w3_raw = load_rows("w3_raw", w3)
         w2_raw = load_rows("w2_raw", w2)
         unit_sb = keep.tile([P, PACK], F32, name="unit_sb")
@@ -93,139 +106,89 @@ def tile_picked_ybloomj_join_p_kernel(tc, x_words, x_scales, w1, w2, unit, w3, o
 
         x_bytes = keep.tile([P, S], U8, name="x_bytes", align_bytes=64)
         nc.vector.tensor_copy(x_bytes[:], table_scales[:].indirect(offs_sb[:]))
-        w1_dealt = [deal("w1_low", w1_raw, 0, nc.vector.tensor_copy), deal("w1_high", w1_raw, 1, nc.vector.tensor_copy)]
-        w1_q = [quantize("w1_%d" % u, w1_dealt[u], 2 * P) for u in range(2)]
-        x_codes = keep.tile([P, S], U32, name="x_codes", align_bytes=64)
+        w1_dealt = [deal("w1_dealt%d" % pair, w1_raw, pair) for pair in range(2)]
+        w1_q = [quantize("w1_%d" % pair, w1_dealt[pair], 2 * P) for pair in range(2)]
+        x_picked = keep.tile([P, S], U32, name="x_picked", align_bytes=64)
         halves = [slice(0, S // 2), slice(S // 2, S)]
         for half in halves:
-            picked = offs_sb[:, half.start // GROUP : half.stop // GROUP]
-            nc.vector.tensor_copy(x_codes[:, half], table_words[:].bitcast(U32).indirect(picked))
-        x_q = (x_codes, x_bytes)
+            nc.vector.tensor_copy(x_picked[:, half], table_words[:].bitcast(U32).indirect(entries(offs_sb, half.start, S // 2)))
+        x_q = (x_picked, x_bytes)
 
         def first_product(w_q, t, cols):
-            acc = psum.tile([P, S], F32, tag="acc", name="acc")
-            product(acc[:, cols], w_q[t // 2], slice(P * (t % 2), P * (t % 2 + 1)), x_q, cols)
-            return acc
+            return product(w_q[t // 2], slice(P * (t % 2), P * (t % 2 + 1)), x_q, cols, cols)
 
-        y = [[(first_product(w1_q, t, cols), cols) for cols in (halves if t == 0 else [slice(0, S)])] for t in range(PACK)]
+        y_cols = [halves] + [[slice(0, S)]] * (PACK - 1)
+        y = [[first_product(w1_q, t, cols) for cols in y_cols[t]] for t in range(PACK)]
 
-        starts = [sum(CHUNKS[:c]) for c in range(len(CHUNKS))]
-        steps = [(c, range(t, t + MERGE[c])) for c in range(len(CHUNKS)) for t in range(0, PACK, MERGE[c])]
-        yv, fetched, hid, grouped, sums = {}, {}, {}, {}, []
-        w3_q = []
+        w3_view, w3_flat = interleaved("w3_grouped", N)
+        nc.vector.tensor_copy(w3_view, by_lines(w3_raw[:]))
+        w3_q = quantize("w3", w3_flat, N)
 
-        def entries(tile, c):
-            return tile[:, starts[c] // GROUP : (starts[c] + CHUNKS[c]) // GROUP]
+        sums = []
 
-        def fetch(s):
-            c, tiles = steps[s]
-            fetched[s] = [keep.tile([P, len(tiles), CHUNKS[c]], F32, name="b%d_%d" % (i, s)) for i in range(3)]
-            if c == 0:
-                for t in tiles:
-                    for acc, cols in y[t]:
-                        nc.scalar.activation(bit[t][:, cols], acc[:, cols], SIGMOID, scale=1.5)
-            order = [(i, t) for first in tiles[::2] for i in range(2) for t in range(first, min(first + 2, tiles.stop))]
-            for i, t in order + [(2, t) for t in tiles]:
-                window = bit[t][:].indirect(entries((h1_sb, h2_sb, h3_sb)[i], c))
-                if i == 2 and PACK * c + t < VECTOR_THIRD:
-                    nc.vector.tensor_copy(fetched[s][i][:, t - tiles.start, :], window)
+        def last_product(hid_flat, start, count):
+            hid_q = quantize("hid_%d" % start, hid_flat, count)
+            sums.append((product(w3_q, slice(0, N), hid_q, slice(0, count), slice(0, count)), start, count))
+
+        def smaller(kept, other):
+            nc.vector.tensor_tensor(kept, kept, other, MIN)
+
+        hid = keep.tile([P, PACK, WIDE], F32, name="hid")
+        wide_bits = []
+
+        def let_through(t):
+            nc.vector.tensor_tensor(hid[:, t, :], value[t][:].indirect(entries(h_sb[0], 0, WIDE)), wide_bits[t][0][:], MULT)
+
+        for t in range(PACK):
+            for acc, cols in zip(y[t], y_cols[t]):
+                nc.scalar.activation(bit[t][:, cols], acc, SIGMOID, scale=1.5)
+            wide_bits.append([keep.tile([P, WIDE], F32, name="wide_bits%d_%d" % (t, i)) for i in range(3)])
+            for i in range(3):
+                looked_up = bit[t][:].indirect(entries(h_sb[i], 0, WIDE))
+                if i == 2 and t < VECTOR_H3:
+                    nc.vector.tensor_copy(wide_bits[t][i][:], looked_up)
                 else:
-                    nc.scalar.activation(fetched[s][i][:, t - tiles.start, :], window, COPY)
+                    nc.scalar.activation(wide_bits[t][i][:], looked_up, COPY)
+            if t == 0:
+                w2_dealt = [deal("w2_dealt%d" % pair, w2_raw, pair) for pair in range(2)]
+                w2_q = [quantize("w2_%d" % pair, w2_dealt[pair], 2 * P) for pair in range(2)]
+                yv = [first_product(w2_q, tt, slice(0, S)) for tt in range(PACK)]
+            else:
+                let_through(t - 1)
+            smaller(wide_bits[t][0][:], wide_bits[t][1][:])
+            if t < VECTOR_VALUES:
+                nc.vector.tensor_scalar(value[t][:, :S], yv[t], unit_sb[:, t : t + 1], None, MULT)
+            else:
+                nc.scalar.activation(value[t][:, :S], yv[t], COPY, scale=unit_sb[:, t : t + 1])
+            smaller(wide_bits[t][0][:], wide_bits[t][2][:])
 
-        def smaller(s, i):
-            nc.vector.tensor_tensor(fetched[s][0][:], fetched[s][0][:], fetched[s][i][:], MIN)
-
-        def let_through(s):
-            c, tiles = steps[s]
-            if tiles.start == 0:
-                hid[c] = keep.tile([P, PACK, CHUNKS[c]], F32, name="hid%d" % c)
-            for t in tiles:
-                nc.vector.tensor_tensor(hid[c][:, t, :], value[t][:].indirect(entries(h1_sb, c)), fetched[s][0][:, t - tiles.start, :], MULT)
-
-        def interleave(name, rows, width):
-            tile = keep.tile([P, width, PACK], BF16, name=name, align_bytes=64)
-            nc.vector.tensor_copy(
-                tile[:].rearrange("p (c i) t -> p c t i", i=4),
-                rows[:].rearrange("p t (c i) -> p c t i", i=4),
-            )
-            return tile[:].rearrange("p c t -> p (c t)")
-
-        def last_product(source, start, width):
-            for first in range(0, width, S):
-                piece = min(S, width - first)
-                hid_q = quantize("hid_%d" % (start + first), source[:, PACK * first : PACK * (first + piece)], piece)
-                acc = psum.tile([P, S], F32, tag="acc", name="acc")
-                done = 0
-                for run in (512, 256, 128):
-                    if piece - done >= run:
-                        product(acc[:, done : done + run], w3_q[0], slice(0, N), hid_q, slice(done, done + run))
-                        done = done + run
-                sums.append((acc, start + first, piece))
-
-        def store(acc, start, width, queue):
-            result = keep.tile([P, width], F32, name="result%d" % start)
-            nc.scalar.copy(result[:], acc[:, :width])
-            queue.dma_start(out[:, start : start + width], result[:])
-
-        def close(c):
-            last_product(grouped[c], starts[c], CHUNKS[c])
-
-        def closes(s):
-            return 0 <= s < len(steps) and steps[s][1].stop == PACK
-
-        w3_q.append(quantize("w3", interleave("w3_grouped", w3_raw, N), N))
-        last = len(steps) - 1
-        for s in range(last):
-            fetch(s)
-            if s == 0:
-                w2_dealt = [deal("w2_%d" % u, w2_raw, u, nc.vector.tensor_copy) for u in range(2)]
-                w2_q = [quantize("w2_%d" % u, w2_dealt[u], 2 * P) for u in range(2)]
-                for t in range(PACK):
-                    yv[t] = first_product(w2_q, t, slice(0, S))
-            if closes(s - 2):
-                close(steps[s - 2][0])
-            if s > 0:
-                let_through(s - 1)
-            smaller(s, 1)
-            if closes(s - 1):
-                c = steps[s - 1][0]
-                grouped[c] = interleave("grouped%d" % c, hid[c], CHUNKS[c])
-            if steps[s][0] == 0:
-                for t in steps[s][1]:
-                    if t < PACK - SCALAR_VALUES:
-                        nc.vector.tensor_scalar(value[t][:, :S], yv[t][:], unit_sb[:, t : t + 1], None, MULT)
-                    else:
-                        nc.scalar.activation(value[t][:, :S], yv[t][:], COPY, scale=unit_sb[:, t : t + 1])
-            smaller(s, 2)
-
-        c = steps[last][0]
-        fetch(last)
-        parts = [(sum(TAIL[:j]), TAIL[j]) for j in range(len(TAIL))]
-        vh = []
-        for first, width in parts:
-            vh.append(keep.tile([P, PACK, width], F32, name="vh%d" % first))
+        narrow_bits = [keep.tile([P, PACK, NARROW], F32, name="narrow_bits%d" % i) for i in range(3)]
+        pairs = [range(0, 2), range(2, PACK)]
+        for i, t in [(i, t) for pair in pairs for i in range(2) for t in pair] + [(2, t) for t in range(PACK)]:
+            nc.scalar.activation(narrow_bits[i][:, t, :], bit[t][:].indirect(entries(h_sb[i], WIDE, NARROW)), COPY)
+        parts = range(0, NARROW, PART)
+        narrow_values = [keep.tile([P, PACK, PART], F32, name="narrow_values%d" % first) for first in parts]
+        for first, values in zip(parts, narrow_values):
             for t in range(PACK):
-                picked = h1_sb[:, (starts[c] + first) // GROUP : (starts[c] + first + width) // GROUP]
-                nc.scalar.activation(vh[-1][:, t, :], value[t][:].indirect(picked), COPY)
-        if closes(last - 2):
-            close(steps[last - 2][0])
-        let_through(last - 1)
-        grouped[c - 1] = interleave("grouped%d" % (c - 1), hid[c - 1], CHUNKS[c - 1])
-        for pair in (slice(0, 2), slice(2, 4)):
-            nc.vector.tensor_tensor(fetched[last][0][:, pair, :], fetched[last][0][:, pair, :], fetched[last][1][:, pair, :], MIN)
-        close(c - 1)
-        smaller(last, 2)
-        tails = []
-        for (first, width), values in zip(parts, vh):
-            tile = keep.tile([P, width, PACK], BF16, name="grouped_last%d" % first, align_bytes=64)
-            nc.vector.tensor_tensor(
-                tile[:].rearrange("p (c i) t -> p c t i", i=4),
-                values[:].rearrange("p t (c i) -> p c t i", i=4),
-                fetched[last][0][:, :, first : first + width].rearrange("p t (c i) -> p c t i", i=4),
-                MULT,
-            )
-            tails.append(tile[:].rearrange("p c t -> p (c t)"))
-        for (first, width), source in zip(parts, tails):
-            last_product(source, starts[c] + first, width)
-        for acc, start, width in sums:
-            store(acc, start, width, nc.sync)
+                nc.scalar.activation(values[:, t, :], value[t][:].indirect(entries(h_sb[0], WIDE + first, PART)), COPY)
+
+        let_through(PACK - 1)
+        wide_view, wide_flat = interleaved("wide_grouped", WIDE)
+        nc.vector.tensor_copy(wide_view, by_lines(hid[:]))
+        for pair in pairs:
+            smaller(narrow_bits[0][:, pair.start : pair.stop, :], narrow_bits[1][:, pair.start : pair.stop, :])
+        for first in range(0, WIDE, BANK):
+            count = min(BANK, WIDE - first)
+            last_product(wide_flat[:, PACK * first : PACK * (first + count)], first, count)
+        smaller(narrow_bits[0][:], narrow_bits[2][:])
+
+        narrow_grouped = [interleaved("narrow_grouped%d" % first, PART) for first in parts]
+        for first, values, (view, flat) in zip(parts, narrow_values, narrow_grouped):
+            nc.vector.tensor_tensor(view, by_lines(values[:]), by_lines(narrow_bits[0][:, :, first : first + PART]), MULT)
+        for first, (view, flat) in zip(parts, narrow_grouped):
+            last_product(flat, WIDE + first, PART)
+
+        for acc, start, count in sums:
+            result = keep.tile([P, count], F32, name="result%d" % start)
+            nc.scalar.copy(result[:], acc)
+            nc.sync.dma_start(out[:, start : start + count], result[:])

from contextlib import ExitStack

import concourse.mybir as mybir

F32 = mybir.dt.float32
BF16 = mybir.dt.bfloat16
I32 = mybir.dt.int32
U32 = mybir.dt.uint32
U16 = mybir.dt.uint16
U8 = mybir.dt.uint8
FP8X4 = mybir.dt.float8_e4m3fn_x4
MULT = mybir.AluOpType.mult
MIN = mybir.AluOpType.min
COPY = mybir.ActivationFunctionType.Copy
SIGMOID = mybir.ActivationFunctionType.Sigmoid

K, T, S, N, H, U = 512, 2048, 512, 128, 512, 1024
FLOPS = 2 * (2 * K * H * S + H * N * U)

P = 128
PACK = 4
QUADRANT = 32
GROUP = 16
BANK = 512
LINE = 4
WIDE = 768
NARROW = U - WIDE
PART = 128
WINDOW = WIDE + GROUP
VECTOR_H3 = 3
VECTOR_VALUES = 3


def tile_picked_ybloomj_join_p_kernel(tc, x_words, x_scales, w1, w2, unit, w3, offs, h1, h2, h3, out):
    nc = tc.nc
    with ExitStack() as ctx:
        lists = ctx.enter_context(tc.tile_pool(name="lists", bufs=1))
        keep = ctx.enter_context(tc.tile_pool(name="keep", bufs=1))
        psum = ctx.enter_context(tc.psum_pool(name="psum", bufs=8))

        def load_list(name, src):
            tile = lists.tile(list(src.shape), U16, name=name)
            nc.sync.dma_start(tile[:], src)
            return tile

        def load_rows(name, src):
            tile = keep.tile([P, PACK, src.shape[1]], F32, name=name)
            nc.sync.dma_start(tile[:], src.rearrange("(p j) c -> p j c", j=PACK))
            return tile

        def entries(list_tile, start, count):
            return list_tile[:, start // GROUP : (start + count) // GROUP]

        def quantize(name, grouped, width):
            words = keep.tile([P, width], U32, name=name + "_words", align_bytes=64)
            scales = keep.tile([P, width], U8, name=name + "_scales", align_bytes=64)
            nc.vector.quantize_mx(out=words[:].bitcast(FP8X4), scales=scales[:], in_=grouped)
            return words, scales

        def deal(name, raw, pair):
            grouped = keep.tile([P, 2, P, PACK], BF16, name=name, align_bytes=64)
            nc.vector.tensor_copy(
                grouped[:].rearrange("p t m j -> p m j t"),
                raw[:].rearrange("p j (m t) -> p m j t", t=PACK)[:, :, :, 2 * pair : 2 * pair + 2],
            )
            return grouped[:].rearrange("p t m j -> p (t m j)")

        def by_lines(rows):
            return rows.rearrange("p t (c i) -> p c t i", i=LINE)

        def interleaved(name, width):
            tile = keep.tile([P, width, PACK], BF16, name=name, align_bytes=64)
            return tile[:].rearrange("p (c i) t -> p c t i", i=LINE), tile[:].rearrange("p c t -> p (c t)")

        def product(lhs, lhs_cols, rhs, rhs_cols, acc_cols):
            acc = psum.tile([P, BANK], F32, tag="acc", name="acc")
            nc.tensor.matmul_mx(
                out=acc[:, acc_cols],
                lhsT=lhs[0][:, lhs_cols].bitcast(FP8X4),
                lhsT_scale=lhs[1][:, lhs_cols],
                rhs=rhs[0][:, rhs_cols].bitcast(FP8X4),
                rhs_scale=rhs[1][:, rhs_cols],
                start=True,
                stop=True,
            )
            return acc[:, acc_cols]

        table_scales = keep.tile([P, T], U8, name="table_scales")
        nc.vector.memset(table_scales[:].bitcast(I32), 0)
        bit = [keep.tile([P, WINDOW], F32, name="bit%d" % t) for t in range(PACK)]
        value = [keep.tile([P, WINDOW], F32, name="value%d" % t) for t in range(PACK)]
        for tile in bit + value:
            nc.vector.memset(tile[:, S:], 0.0)

        offs_sb = load_list("offs_sb", offs)
        for r in range(PACK):
            nc.sync.dma_start(table_scales[r:P:QUADRANT, :].bitcast(I32), x_scales[0, r : K // 32 : PACK, :].bitcast(I32))
        w1_raw = load_rows("w1_raw", w1)
        table_words = keep.tile([P, T], I32, name="table_words")
        nc.sync.dma_start(table_words[:], x_words[0].rearrange("p c r -> p (c r)").bitcast(I32))
        h_sb = [load_list("h1_sb", h1), load_list("h2_sb", h2), load_list("h3_sb", h3)]
        w3_raw = load_rows("w3_raw", w3)
        w2_raw = load_rows("w2_raw", w2)
        unit_sb = keep.tile([P, PACK], F32, name="unit_sb")
        nc.sync.dma_start(unit_sb[:], unit.rearrange("(p t) o -> p (t o)", t=PACK))

        x_bytes = keep.tile([P, S], U8, name="x_bytes", align_bytes=64)
        nc.vector.tensor_copy(x_bytes[:], table_scales[:].indirect(offs_sb[:]))
        w1_dealt = [deal("w1_dealt%d" % pair, w1_raw, pair) for pair in range(2)]
        w1_q = [quantize("w1_%d" % pair, w1_dealt[pair], 2 * P) for pair in range(2)]
        x_picked = keep.tile([P, S], U32, name="x_picked", align_bytes=64)
        halves = [slice(0, S // 2), slice(S // 2, S)]
        for half in halves:
            nc.vector.tensor_copy(x_picked[:, half], table_words[:].bitcast(U32).indirect(entries(offs_sb, half.start, S // 2)))
        x_q = (x_picked, x_bytes)

        def first_product(w_q, t, cols):
            return product(w_q[t // 2], slice(P * (t % 2), P * (t % 2 + 1)), x_q, cols, cols)

        y_cols = [halves] + [[slice(0, S)]] * (PACK - 1)
        y = [[first_product(w1_q, t, cols) for cols in y_cols[t]] for t in range(PACK)]

        w3_view, w3_flat = interleaved("w3_grouped", N)
        nc.vector.tensor_copy(w3_view, by_lines(w3_raw[:]))
        w3_q = quantize("w3", w3_flat, N)

        sums = []

        def last_product(hid_flat, start, count):
            hid_q = quantize("hid_%d" % start, hid_flat, count)
            sums.append((product(w3_q, slice(0, N), hid_q, slice(0, count), slice(0, count)), start, count))

        def smaller(kept, other):
            nc.vector.tensor_tensor(kept, kept, other, MIN)

        hid = keep.tile([P, PACK, WIDE], F32, name="hid")
        wide_bits = []

        def let_through(t):
            nc.vector.tensor_tensor(hid[:, t, :], value[t][:].indirect(entries(h_sb[0], 0, WIDE)), wide_bits[t][0][:], MULT)

        for t in range(PACK):
            for acc, cols in zip(y[t], y_cols[t]):
                nc.scalar.activation(bit[t][:, cols], acc, SIGMOID, scale=1.5)
            wide_bits.append([keep.tile([P, WIDE], F32, name="wide_bits%d_%d" % (t, i)) for i in range(3)])
            for i in range(3):
                looked_up = bit[t][:].indirect(entries(h_sb[i], 0, WIDE))
                if i == 2 and t < VECTOR_H3:
                    nc.vector.tensor_copy(wide_bits[t][i][:], looked_up)
                else:
                    nc.scalar.activation(wide_bits[t][i][:], looked_up, COPY)
            if t == 0:
                w2_dealt = [deal("w2_dealt%d" % pair, w2_raw, pair) for pair in range(2)]
                w2_q = [quantize("w2_%d" % pair, w2_dealt[pair], 2 * P) for pair in range(2)]
                yv = [first_product(w2_q, tt, slice(0, S)) for tt in range(PACK)]
            else:
                let_through(t - 1)
            smaller(wide_bits[t][0][:], wide_bits[t][1][:])
            if t < VECTOR_VALUES:
                nc.vector.tensor_scalar(value[t][:, :S], yv[t], unit_sb[:, t : t + 1], None, MULT)
            else:
                nc.scalar.activation(value[t][:, :S], yv[t], COPY, scale=unit_sb[:, t : t + 1])
            smaller(wide_bits[t][0][:], wide_bits[t][2][:])

        narrow_bits = [keep.tile([P, PACK, NARROW], F32, name="narrow_bits%d" % i) for i in range(3)]
        pairs = [range(0, 2), range(2, PACK)]
        for i, t in [(i, t) for pair in pairs for i in range(2) for t in pair] + [(2, t) for t in range(PACK)]:
            nc.scalar.activation(narrow_bits[i][:, t, :], bit[t][:].indirect(entries(h_sb[i], WIDE, NARROW)), COPY)
        parts = range(0, NARROW, PART)
        narrow_values = [keep.tile([P, PACK, PART], F32, name="narrow_values%d" % first) for first in parts]
        for first, values in zip(parts, narrow_values):
            for t in range(PACK):
                nc.scalar.activation(values[:, t, :], value[t][:].indirect(entries(h_sb[0], WIDE + first, PART)), COPY)

        let_through(PACK - 1)
        wide_view, wide_flat = interleaved("wide_grouped", WIDE)
        nc.vector.tensor_copy(wide_view, by_lines(hid[:]))
        for pair in pairs:
            smaller(narrow_bits[0][:, pair.start : pair.stop, :], narrow_bits[1][:, pair.start : pair.stop, :])
        for first in range(0, WIDE, BANK):
            count = min(BANK, WIDE - first)
            last_product(wide_flat[:, PACK * first : PACK * (first + count)], first, count)
        smaller(narrow_bits[0][:], narrow_bits[2][:])

        narrow_grouped = [interleaved("narrow_grouped%d" % first, PART) for first in parts]
        for first, values, (view, flat) in zip(parts, narrow_values, narrow_grouped):
            nc.vector.tensor_tensor(view, by_lines(values[:]), by_lines(narrow_bits[0][:, :, first : first + PART]), MULT)
        for first, (view, flat) in zip(parts, narrow_grouped):
            last_product(flat, WIDE + first, PART)

        for acc, start, count in sums:
            result = keep.tile([P, count], F32, name="result%d" % start)
            nc.scalar.copy(result[:], acc)
            nc.sync.dma_start(out[:, start : start + count], result[:])
